import numpy as np
import ml_dtypes


def mxq(x, axis, fmt="e4m3"):
    dtype, down = {"e4m3": (ml_dtypes.float8_e4m3fn, 7), "e5m2": (ml_dtypes.float8_e5m2, 14)}[fmt]
    v = np.moveaxis(np.asarray(x, np.float32).astype(ml_dtypes.bfloat16).astype(np.float64), axis, -1)
    blocks = v.reshape(v.shape[:-1] + (-1, 32))
    amax = np.abs(blocks).max(-1, keepdims=True)
    byte = np.maximum(np.where(amax > 0, np.frexp(amax)[1] - 1 + 127, 0) - down, 1)
    scale = np.exp2(byte - 127.0)
    codes = (blocks / scale).astype(np.float32).astype(dtype).astype(np.float64)
    return np.moveaxis((codes * scale).reshape(v.shape), -1, axis)


WIDE = False


def mx_kscale(k):
    if not WIDE:
        return np.ones(k)
    levels = np.array([30, -30])
    if k % 512:
        return np.exp2(np.random.permutation(np.resize(levels, k // 32))).repeat(32)
    a = np.empty((k // 512, 16))
    for p in range(k // 512):
        a[p, :8] = np.random.permutation(np.resize(levels, 8))
        for g in range(8):
            far = levels[np.abs(levels - a[p, g]) >= 10]
            a[p, g + 8] = far[np.random.randint(len(far))]
    return np.exp2(a.ravel()).repeat(32)


BF16 = ml_dtypes.bfloat16


def bf(x):
    return np.asarray(x, np.float32).astype(BF16)


def f64(x):
    return np.asarray(x).astype(np.float64)


E2M1 = np.array([0.0, 0.5, 1.0, 1.5, 2.0, 3.0, 4.0, 6.0, -0.0, -0.5, -1.0, -1.5, -2.0, -3.0, -4.0, -6.0])


def pack_weight(w, fmt):
    k, n = w.shape
    w = f64(bf(w)).reshape(k // 32, 32, n)
    amax = np.abs(w).max(1)
    if fmt == "e4m3":
        byte = np.frexp(amax)[1] - 1 + 127 - 7
    else:
        mant, ex = np.frexp(amax / 6.0)
        byte = np.where(mant > 0.5, ex, ex - 1) + 127
    byte = np.clip(np.where(amax > 0, byte, 1), 1, 254)
    scaled = (w * np.exp2(127.0 - byte)[:, None, :]).reshape(k, n).astype(np.float32)
    by_word = np.ascontiguousarray(scaled.reshape(k // 512, 128, 4, n).transpose(0, 1, 3, 2))
    if fmt == "e4m3":
        words = by_word.astype(ml_dtypes.float8_e4m3fn).view(np.uint8)
    else:
        c = by_word.astype(ml_dtypes.float4_e2m1fn).view(np.uint8) & 0xF
        words = c[..., 0::2] | (c[..., 1::2] << 4)
    return np.ascontiguousarray(words), np.ascontiguousarray(byte.astype(np.uint8).reshape(k // 512, 16, n))


def unpack_weight(words, scales, fmt):
    g, p, n, _ = words.shape
    if fmt == "e4m3":
        vals = np.ascontiguousarray(words).view(ml_dtypes.float8_e4m3fn).astype(np.float64)
    else:
        nib = np.empty((g, p, n, 4), np.uint8)
        nib[..., 0::2] = words & 0xF
        nib[..., 1::2] = words >> 4
        vals = E2M1[nib]
    vals = vals * np.repeat(np.exp2(scales.astype(np.float64) - 127.0), 8, axis=1)[..., None]
    return vals.transpose(0, 1, 3, 2).reshape(g * 512, n)
def pack4(w):
    words, scales = pack_weight(w, "e2m1")
    return words.reshape(words.shape[0], 128, -1), scales


def unpack4(words, scales):
    return unpack_weight(words.reshape(words.shape[0], 128, -1, 2), scales, "e2m1")


M, D, E, V = 512, 2048, 1024, 2048


def setup_inputs():
    s = mx_kscale(D)
    t = mx_kscale(E)
    near_words, near_scales = pack4(np.random.standard_normal((D, E)) / np.sqrt(D) / s[:, None] * t)
    far_words, far_scales = pack4(np.random.standard_normal((D, E)) / np.sqrt(D) / s[:, None] * t)
    return {"x": bf(np.random.standard_normal((M, D)) * s),
            "near_words": near_words,
            "near_scales": near_scales,
            "near_bias": bf(0.3 * np.random.standard_normal(E) * t),
            "far_words": far_words,
            "far_scales": far_scales,
            "far_bias": bf(0.3 * np.random.standard_normal(E) * t),
            "table": bf(np.random.standard_normal((V, E)) / np.sqrt(E) / t),
            "vocab_bias": bf(0.5 * np.random.standard_normal(V))}


def reference(x, near_words, near_scales, near_bias, far_words, far_scales, far_bias, table, vocab_bias):
    xq = mxq(f64(x), 1, "e4m3")
    near = np.maximum((xq @ unpack4(near_words, near_scales)) + f64(near_bias), 0.0)
    far = np.maximum((xq @ unpack4(far_words, far_scales)) + f64(far_bias), 0.0)
    tq = mxq(f64(table), 1, "e4m3")
    c = f64(vocab_bias)
    near_logits = (mxq(near, 1, "e5m2") @ tq.T) + c
    far_logits = (mxq(far, 1, "e5m2") @ tq.T) + c
    return near_logits, far_logits

@@ -1,0 +1,414 @@
+from contextlib import ExitStack
+
+import concourse.mybir as mybir
+from concourse.masks import make_identity
+
+M, D, E, V = 512, 2048, 1024, 2048
+FLOPS = 2 * 2 * M * D * E + 2 * 2 * M * E * V
+
+F32 = mybir.dt.float32
+BF16 = mybir.dt.bfloat16
+I32 = mybir.dt.int32
+U32 = mybir.dt.uint32
+U8 = mybir.dt.uint8
+E4M3 = mybir.dt.float8_e4m3fn_x4
+E5M2 = mybir.dt.float8_e5m2_x4
+E2M1 = mybir.dt.float4_e2m1fn_x4
+ADD = mybir.AluOpType.add
+MULT = mybir.AluOpType.mult
+RELU = mybir.ActivationFunctionType.Relu
+
+P = 128
+XG = D // 512
+EG = E // 512
+VN = V // 512
+MT = M // 128
+
+
+def tile_tied_vocabulary_head_s9_kernel(
+    tc, x, near_words, near_scales, near_bias, far_words, far_scales, far_bias, table, vocab_bias, out_0, out_1
+):
+    nc = tc.nc
+    words = (near_words, far_words)
+    scales = (near_scales, far_scales)
+    biases = (near_bias, far_bias)
+    outs = (out_0, out_1)
+
+    with ExitStack() as ctx:
+        keep = ctx.enter_context(tc.tile_pool(name="keep", bufs=1))
+        flow = ctx.enter_context(tc.tile_pool(name="flow", bufs=2))
+        psum = ctx.enter_context(tc.psum_pool(name="psum", bufs=8))
+        ctx.enter_context(tc.manual_schedule())
+
+        ident = keep.tile([P, P], F32, align_bytes=64)
+        x_raw = keep.tile([P, XG, MT, 512], BF16, align_bytes=64)
+        x_codes = keep.tile([P, XG, M], U32, align_bytes=64)
+        x_planes = keep.tile([P, XG, M], U8, align_bytes=64)
+        w_raw = keep.tile([P, 2, XG, 2 * E], U8, align_bytes=64)
+        w_codes = keep.tile([P, 2, XG, 2 * E], U8, align_bytes=64)
+        s_raw = keep.tile([P, 2, XG, E], U8, align_bytes=64)
+        s_planes = keep.tile([P, 2, XG, E], U8, align_bytes=64)
+        t_codes = keep.tile([P, VN, EG, 512], U32, align_bytes=64)
+        t_planes = keep.tile([P, VN, EG, 512], U8, align_bytes=64)
+        h_codes = keep.tile([P, 2, EG, M], U32, align_bytes=64)
+        h_planes = keep.tile([P, 2, EG, M], U8, align_bytes=64)
+        vbias = keep.tile([P, V], BF16, align_bytes=64)
+        brow = keep.tile([P, P], BF16, align_bytes=64)
+        brow32 = keep.tile([P, P], F32, align_bytes=64)
+        bcol = keep.tile([P, 4 * EG], F32, align_bytes=64)
+        bcol2 = keep.tile([P, 4 * EG], F32, align_bytes=64)
+        warm = keep.tile([P, 1], F32, align_bytes=64)
+        bcols = (bcol, bcol2)
+
+        def load_x(g):
+            nc.sync.dma_start(
+                out=x_raw[:, g, :, :], in_=x[:, 512 * g : 512 * g + 512].rearrange("(r p) k -> p r k", p=P)
+            )
+
+        def load_words(h, g0, n):
+            nc.sync.dma_start(
+                out=w_raw[:, h, g0 : g0 + n, :].bitcast(I32),
+                in_=words[h][g0 : g0 + n].rearrange("g p c -> p g c").bitcast(I32),
+            )
+
+        def load_scales(h):
+            for q in range(4):
+                nc.sync.dma_start(
+                    out=s_raw[32 * q : 32 * q + 4, h, :, :].bitcast(I32),
+                    in_=scales[h][:, 4 * q : 4 * q + 4, :].rearrange("g r n -> r g n").bitcast(I32),
+                )
+
+        t_raw = {}
+
+        def load_table(n):
+            raw = flow.tile([P, 4, E], BF16, name="t_raw", bufs=4, align_bytes=64)
+            nc.sync.dma_start(out=raw[:], in_=table[512 * n : 512 * n + 512, :].rearrange("(r p) k -> p r k", p=P))
+            t_raw[n] = raw
+
+        nc.vector.memset(warm[:], 0.0)
+        nc.scalar.activation(out=warm[:], in_=warm[:], func=RELU)
+        nc.vector.memset(s_raw[:, 0, :, :].rearrange("p g n -> p (g n)").bitcast(I32), 0)
+        make_identity(nc, ident[:])
+        nc.vector.memset(brow32[:], 0.0)
+        nc.vector.memset(s_raw[:, 1, :, :].rearrange("p g n -> p (g n)").bitcast(I32), 0)
+        load_x(0)
+        load_x(1)
+        load_x(2)
+        load_scales(0)
+        load_words(0, 0, 1)
+        load_x(3)
+        load_words(0, 1, 1)
+        load_words(0, 2, 2)
+        load_table(0)
+        load_scales(1)
+        load_words(1, 0, 4)
+        load_table(1)
+        load_table(2)
+        nc.sync.dma_start(out=vbias[:], in_=vocab_bias.partition_broadcast(P))
+        load_table(3)
+        for h in range(2):
+            for e in range(EG):
+                row = 8 * h + 4 * e
+                nc.gpsimd.dma_start(
+                    out=brow[row : row + 4, :].rearrange("t (b i) -> t b i", i=8),
+                    in_=biases[h][512 * e : 512 * e + 512].rearrange("(b t i) -> t b i", t=4, i=8),
+                )
+
+        def perm_words(h, e, g, eng):
+            eng.tensor_copy(
+                out=w_codes[:, h, g, 1024 * e : 1024 * e + 1024].bitcast(I32).rearrange("p (t b w) -> p t b w", t=4, b=16),
+                in_=w_raw[:, h, g, 1024 * e : 1024 * e + 1024].bitcast(I32).rearrange("p (b t w) -> p t b w", t=4, b=16),
+            )
+
+        def perm_scales(h, t, eng):
+            src = s_raw[:, h, :, :].rearrange("p g n -> p (g n)").bitcast(I32)
+            dst = s_planes[:, h, :, :].rearrange("p g n -> p (g n)").bitcast(I32)
+            eng.tensor_copy(
+                out=dst.rearrange("p (c t b w) -> p c t b w", t=4, b=16, w=2)[:, :, t],
+                in_=src.rearrange("p (c b t w) -> p c t b w", t=4, b=16, w=2)[:, :, t],
+            )
+
+        def bank(name):
+            return psum.tile([P, 512], F32, name=name, tag="bank", bufs=8)
+
+        x_banks = {}
+
+        def x_transpose(g):
+            w = x_raw[:, g, :, :].rearrange("p r k -> p (r k)").bitcast(F32)
+            for rp in range(2):
+                b = bank("x_bank")
+                for r in range(2):
+                    for u in range(2):
+                        o = 256 * (2 * rp + r)
+                        nc.tensor.transpose(
+                            b[:, 128 * (2 * r + u) : 128 * (2 * r + u) + 128], w[:, o + u : o + 256 : 2], ident[:]
+                        )
+                x_banks[g, rp] = b
+
+        x_grouped = {}
+
+        def x_copy(g):
+            grouped = flow.tile([P, 2048], BF16, name="x_grouped", bufs=3, align_bytes=64)
+            for rp in range(2):
+                dst = grouped[:, 1024 * rp : 1024 * rp + 1024].bitcast(F32).rearrange("p (r n u) -> p r n u", r=2, u=2)
+                src = x_banks[g, rp][:].rearrange("p (r u n) -> p r n u", r=2, u=2)
+                if rp == 0:
+                    nc.scalar.copy(out=dst, in_=src)
+                else:
+                    nc.vector.tensor_copy(out=dst, in_=src)
+            x_grouped[g] = grouped
+
+        def x_quant(g):
+            nc.vector.quantize_mx(out=x_codes[:, g, :].bitcast(E4M3), scales=x_planes[:, g, :], in_=x_grouped[g][:])
+
+        s1_banks = {}
+
+        def s1(h, e, g, ts):
+            for t in ts:
+                if g == 0:
+                    s1_banks[h, e, t] = bank("s1_bank")
+                c = 512 * e + 128 * t
+                nc.tensor.matmul_mx(
+                    out=s1_banks[h, e, t][:],
+                    lhsT=w_codes[:, h, g, 2 * c : 2 * c + 256].bitcast(E2M1),
+                    lhsT_scale=s_planes[:, h, g, c : c + 128],
+                    rhs=x_codes[:, g, :].bitcast(E4M3),
+                    rhs_scale=x_planes[:, g, :],
+                    start=(g == 0),
+                    stop=(g == XG - 1),
+                )
+
+        planes = {}
+
+        def relu(h, e, t):
+            if t == 0:
+                planes[h, e] = flow.tile([P, 4, M], BF16, name="planes", bufs=2, align_bytes=64)
+            nc.scalar.activation(
+                out=planes[h, e][:, t, :], in_=s1_banks[h, e, t][:], func=RELU, bias=bcols[h][:, 4 * e + t : 4 * e + t + 1]
+            )
+
+        grouped_h = {}
+
+        def h_inter(h, e, half, eng):
+            if half == 0:
+                grouped_h[h, e] = flow.tile([P, M, 4], BF16, name="h_grouped", bufs=2, align_bytes=64)
+            a = 256 * half
+            dst = grouped_h[h, e][:, a : a + 256, :]
+            src = planes[h, e][:, :, a : a + 256].rearrange("p t n -> p n t")
+            if eng == 0:
+                nc.vector.tensor_copy(out=dst, in_=src)
+            else:
+                nc.scalar.copy(out=dst, in_=src)
+
+        def h_quant(h, e, half):
+            a = 256 * half
+            nc.vector.quantize_mx(
+                out=h_codes[:, h, e, a : a + 256].bitcast(E5M2),
+                scales=h_planes[:, h, e, a : a + 256],
+                in_=grouped_h[h, e][:, a : a + 256, :].rearrange("p n t -> p (n t)"),
+            )
+
+        t_perm = {}
+
+        def perm_table(n, u, half, eng):
+            if (u, half) == (0, 0):
+                t_perm[n] = flow.tile([P, 2, 2048], BF16, name="t_perm", bufs=3, align_bytes=64)
+            src = t_raw[n][:].rearrange("p r k -> p (r k)").rearrange("p (c u e i) -> p c u i e", u=2, e=2, i=8)
+            dst = t_perm[n][:].rearrange("p u (c i e) -> p c u i e", i=8, e=2)
+            dst = dst[:, 64 * half : 64 * half + 64, u]
+            src = src[:, 64 * half : 64 * half + 64, u]
+            if eng == 0:
+                nc.vector.tensor_copy(out=dst, in_=src)
+            elif eng == 1:
+                nc.scalar.copy(out=dst, in_=src)
+            else:
+                nc.gpsimd.tensor_scalar(out=dst, in0=src, scalar1=1.0, scalar2=0.0, op0=MULT, op1=ADD)
+
+        t_banks = {}
+
+        def t_transpose(n, rp):
+            for e in range(EG):
+                b = bank("t_bank")
+                for r in range(2):
+                    for u in range(2):
+                        o = 256 * (2 * rp + r) + 128 * e
+                        nc.tensor.transpose(
+                            b[:, 128 * (2 * r + u) : 128 * (2 * r + u) + 128],
+                            t_perm[n][:, u, :].bitcast(F32)[:, o : o + 128],
+                            ident[:],
+                        )
+                t_banks[n, e, rp] = b
+
+        t_grouped = {}
+
+        def t_copy(n, rp, e, eng):
+            if rp == 0:
+                t_grouped[n, e] = flow.tile([P, 2048], BF16, name="t_grouped", bufs=4, align_bytes=64)
+            dst = t_grouped[n, e][:, 1024 * rp : 1024 * rp + 1024].bitcast(F32).rearrange("p (r n u) -> p r n u", r=2, u=2)
+            src = t_banks[n, e, rp][:].rearrange("p (r u n) -> p r n u", r=2, u=2)
+            if eng == 0:
+                nc.vector.tensor_copy(out=dst, in_=src)
+            else:
+                nc.scalar.copy(out=dst, in_=src)
+
+        def t_quant(n, e):
+            nc.vector.quantize_mx(
+                out=t_codes[:, n, e, :].bitcast(E4M3), scales=t_planes[:, n, e, :], in_=t_grouped[n, e][:]
+            )
+
+        s2_banks = {}
+
+        def s2(h, n, m):
+            b = bank("s2_bank")
+            for e in range(EG):
+                nc.tensor.matmul_mx(
+                    out=b[:],
+                    lhsT=h_codes[:, h, e, 128 * m : 128 * m + 128].bitcast(E5M2),
+                    lhsT_scale=h_planes[:, h, e, 128 * m : 128 * m + 128],
+                    rhs=t_codes[:, n, e, :].bitcast(E4M3),
+                    rhs_scale=t_planes[:, n, e, :],
+                    start=(e == 0),
+                    stop=(e == EG - 1),
+                )
+            s2_banks[h, n, m] = b
+
+        def finish(h, n, m):
+            res = flow.tile([P, 512], F32, name="res", bufs=8, align_bytes=64)
+            nc.vector.tensor_tensor(
+                out=res[:], in0=s2_banks[h, n, m][:], in1=vbias[:, 512 * n : 512 * n + 512], op=ADD
+            )
+            nc.sync.dma_start(out=outs[h][128 * m : 128 * m + 128, 512 * n : 512 * n + 512], in_=res[:])
+
+        T4 = range(4)
+        DVE, ACT, POOL = 0, 1, 2
+        x_transpose(0)
+        x_copy(0)
+        x_transpose(1)
+        x_quant(0)
+        x_copy(1)
+        for t in T4:
+            perm_scales(0, t, nc.vector)
+        perm_words(0, 0, 0, nc.vector)
+        x_transpose(2)
+        x_quant(1)
+        x_copy(2)
+        x_quant(2)
+        s1(0, 0, 0, T4)
+        x_transpose(3)
+        nc.vector.tensor_copy(out=brow32[0:16, :], in_=brow[0:16, :])
+        bias_bank = bank("bias_bank")
+        nc.tensor.transpose(bias_bank[:, 0:128], brow32[:], ident[:])
+        perm_words(0, 0, 1, nc.vector)
+        x_copy(3)
+        nc.scalar.copy(out=bcol[:], in_=bias_bank[:, 0:8])
+        nc.scalar.copy(out=bcol2[:], in_=bias_bank[:, 8:16])
+        perm_words(0, 0, 2, nc.vector)
+        x_quant(3)
+        perm_words(0, 0, 3, nc.vector)
+        s1(0, 0, 1, T4)
+        s1(0, 0, 2, T4)
+        s1(0, 0, 3, T4)
+        for g in range(4):
+            perm_words(0, 1, g, nc.vector)
+        perm_table(0, 0, 0, ACT)
+        perm_table(0, 1, 0, DVE)
+        perm_table(0, 0, 1, ACT)
+        perm_table(0, 1, 1, DVE)
+        for t in T4:
+            for g in range(4):
+                s1(0, 1, g, [t])
+            relu(0, 0, t)
+        for t in T4:
+            perm_scales(1, t, nc.vector)
+        for g in range(4):
+            perm_words(1, 0, g, nc.vector)
+        perm_table(1, 0, 0, POOL)
+        perm_table(1, 1, 0, ACT)
+        perm_table(1, 0, 1, POOL)
+        perm_table(1, 1, 1, DVE)
+        t_transpose(0, 0)
+        t_transpose(0, 1)
+        for half in range(2):
+            h_inter(0, 0, half, DVE)
+        for rp in range(2):
+            for e in range(2):
+                t_copy(0, rp, e, ACT)
+        for half in range(2):
+            h_quant(0, 0, half)
+        for t in T4:
+            relu(0, 1, t)
+        for e in range(2):
+            t_quant(0, e)
+        for g in range(4):
+            s1(1, 0, g, T4)
+        for g in range(4):
+            perm_words(1, 1, g, nc.vector)
+        perm_table(2, 0, 0, DVE)
+        perm_table(2, 1, 0, DVE)
+        t_transpose(1, 0)
+        t_transpose(1, 1)
+        for half in range(2):
+            h_inter(0, 1, half, DVE)
+        for rp in range(2):
+            for e in range(2):
+                t_copy(1, rp, e, ACT)
+        for half in range(2):
+            h_quant(0, 1, half)
+        perm_table(2, 0, 1, DVE)
+        perm_table(2, 1, 1, DVE)
+        for t in T4:
+            relu(1, 0, t)
+        for e in range(2):
+            t_quant(1, e)
+        perm_table(3, 0, 0, POOL)
+        perm_table(3, 1, 0, POOL)
+        perm_table(3, 0, 1, POOL)
+        for i in range(8):
+            n, m = divmod(i, 4)
+            t, half = divmod(i, 2)
+            s1(1, 1, 2 * half, [t])
+            s1(1, 1, 2 * half + 1, [t])
+            s2(0, n, m)
+            finish(0, n, m)
+            if half == 1 and t > 0:
+                relu(1, 1, t - 1)
+            if i == 0:
+                h_inter(1, 0, 0, ACT)
+            if i == 1:
+                h_inter(1, 0, 1, DVE)
+            if i == 3:
+                h_quant(1, 0, 0)
+                h_quant(1, 0, 1)
+                t_transpose(2, 0)
+                t_transpose(2, 1)
+                for rp in range(2):
+                    for e in range(2):
+                        t_copy(2, rp, e, ACT)
+            if i == 4:
+                perm_table(3, 1, 1, ACT)
+            if i == 7:
+                t_quant(2, 0)
+                t_quant(2, 1)
+        relu(1, 1, 3)
+        t_transpose(3, 0)
+        t_transpose(3, 1)
+        h_inter(1, 1, 0, DVE)
+        for rp in range(2):
+            for e in range(2):
+                t_copy(3, rp, e, ACT)
+        for m in range(4):
+            s2(0, 2, m)
+            finish(0, 2, m)
+            if m == 2:
+                t_quant(3, 0)
+                t_quant(3, 1)
+        h_inter(1, 1, 1, ACT)
+        for half in range(2):
+            h_quant(1, 1, half)
+        for m in range(4):
+            s2(0, 3, m)
+            finish(0, 3, m)
+        for n in range(4):
+            for m in range(4):
+                s2(1, n, m)
+                finish(1, n, m)

@@ -60,9 +60,10 @@ def tile_tied_vocabulary_head_s9_kernel(
         warm = keep.tile([P, 1], F32, align_bytes=64)
         bcols = (bcol, bcol2)
 
-        def load_x(g):
+        def load_x(g, r0, n):
             nc.sync.dma_start(
-                out=x_raw[:, g, :, :], in_=x[:, 512 * g : 512 * g + 512].rearrange("(r p) k -> p r k", p=P)
+                out=x_raw[:, g, r0 : r0 + n, :],
+                in_=x[P * r0 : P * (r0 + n), 512 * g : 512 * g + 512].rearrange("(r p) k -> p r k", p=P),
             )
 
         def load_words(h, g0, n):
@@ -91,12 +92,14 @@ def tile_tied_vocabulary_head_s9_kernel(
         make_identity(nc, ident[:])
         nc.vector.memset(brow32[:], 0.0)
         nc.vector.memset(s_raw[:, 1, :, :].rearrange("p g n -> p (g n)").bitcast(I32), 0)
-        load_x(0)
-        load_x(1)
-        load_x(2)
+        load_x(0, 0, 2)
+        load_x(0, 2, 2)
+        load_x(1, 0, 4)
         load_scales(0)
+        load_x(2, 0, 4)
+        load_x(3, 0, 2)
+        load_x(3, 2, 2)
         load_words(0, 0, 1)
-        load_x(3)
         load_words(0, 1, 1)
         load_words(0, 2, 2)
         load_table(0)
@@ -114,18 +117,18 @@ def tile_tied_vocabulary_head_s9_kernel(
                     in_=biases[h][512 * e : 512 * e + 512].rearrange("(b t i) -> t b i", t=4, i=8),
                 )
 
-        def perm_words(h, e, g, eng):
-            eng.tensor_copy(
-                out=w_codes[:, h, g, 1024 * e : 1024 * e + 1024].bitcast(I32).rearrange("p (t b w) -> p t b w", t=4, b=16),
-                in_=w_raw[:, h, g, 1024 * e : 1024 * e + 1024].bitcast(I32).rearrange("p (b t w) -> p t b w", t=4, b=16),
+        def perm_words(h, e, g, n):
+            nc.vector.tensor_copy(
+                out=w_codes[:, h, g : g + n, 1024 * e : 1024 * e + 1024].bitcast(I32).rearrange("p g (t b w) -> p g t b w", t=4, b=16),
+                in_=w_raw[:, h, g : g + n, 1024 * e : 1024 * e + 1024].bitcast(I32).rearrange("p g (b t w) -> p g t b w", t=4, b=16),
             )
 
-        def perm_scales(h, t, eng):
+        def perm_scales(h):
             src = s_raw[:, h, :, :].rearrange("p g n -> p (g n)").bitcast(I32)
             dst = s_planes[:, h, :, :].rearrange("p g n -> p (g n)").bitcast(I32)
-            eng.tensor_copy(
-                out=dst.rearrange("p (c t b w) -> p c t b w", t=4, b=16, w=2)[:, :, t],
-                in_=src.rearrange("p (c b t w) -> p c t b w", t=4, b=16, w=2)[:, :, t],
+            nc.vector.tensor_copy(
+                out=dst.rearrange("p (c t b w) -> p c t b w", t=4, b=16, w=2),
+                in_=src.rearrange("p (c b t w) -> p c t b w", t=4, b=16, w=2),
             )
 
         def bank(name):
@@ -133,30 +136,28 @@ def tile_tied_vocabulary_head_s9_kernel(
 
         x_banks = {}
 
-        def x_transpose(g):
+        def x_transpose(g, rp):
             w = x_raw[:, g, :, :].rearrange("p r k -> p (r k)").bitcast(F32)
-            for rp in range(2):
-                b = bank("x_bank")
-                for r in range(2):
-                    for u in range(2):
-                        o = 256 * (2 * rp + r)
-                        nc.tensor.transpose(
-                            b[:, 128 * (2 * r + u) : 128 * (2 * r + u) + 128], w[:, o + u : o + 256 : 2], ident[:]
-                        )
-                x_banks[g, rp] = b
+            b = bank("x_bank")
+            for r in range(2):
+                for u in range(2):
+                    o = 256 * (2 * rp + r)
+                    nc.tensor.transpose(
+                        b[:, 128 * (2 * r + u) : 128 * (2 * r + u) + 128], w[:, o + u : o + 256 : 2], ident[:]
+                    )
+            x_banks[g, rp] = b
 
         x_grouped = {}
 
-        def x_copy(g):
-            grouped = flow.tile([P, 2048], BF16, name="x_grouped", bufs=3, align_bytes=64)
-            for rp in range(2):
-                dst = grouped[:, 1024 * rp : 1024 * rp + 1024].bitcast(F32).rearrange("p (r n u) -> p r n u", r=2, u=2)
-                src = x_banks[g, rp][:].rearrange("p (r u n) -> p r n u", r=2, u=2)
-                if rp == 0:
-                    nc.scalar.copy(out=dst, in_=src)
-                else:
-                    nc.vector.tensor_copy(out=dst, in_=src)
-            x_grouped[g] = grouped
+        def x_copy(g, rp, eng):
+            if rp == 0:
+                x_grouped[g] = flow.tile([P, 2048], BF16, name="x_grouped", bufs=3, align_bytes=64)
+            dst = x_grouped[g][:, 1024 * rp : 1024 * rp + 1024].bitcast(F32).rearrange("p (r n u) -> p r n u", r=2, u=2)
+            src = x_banks[g, rp][:].rearrange("p (r u n) -> p r n u", r=2, u=2)
+            if eng == 0:
+                nc.vector.tensor_copy(out=dst, in_=src)
+            else:
+                nc.scalar.copy(out=dst, in_=src)
 
         def x_quant(g):
             nc.vector.quantize_mx(out=x_codes[:, g, :].bitcast(E4M3), scales=x_planes[:, g, :], in_=x_grouped[g][:])
@@ -272,143 +273,146 @@ def tile_tied_vocabulary_head_s9_kernel(
                 )
             s2_banks[h, n, m] = b
 
-        def finish(h, n, m):
-            res = flow.tile([P, 512], F32, name="res", bufs=8, align_bytes=64)
-            nc.vector.tensor_tensor(
-                out=res[:], in0=s2_banks[h, n, m][:], in1=vbias[:, 512 * n : 512 * n + 512], op=ADD
-            )
-            nc.sync.dma_start(out=outs[h][128 * m : 128 * m + 128, 512 * n : 512 * n + 512], in_=res[:])
+        res_tiles = {}
+
+        def finish(h, n, m, eng=0):
+            if n % 2 == 0:
+                res_tiles[h, n, m] = flow.tile([P, 1024], F32, name="res", bufs=6, align_bytes=64)
+            res = res_tiles[h, n - n % 2, m]
+            c = 512 * (n % 2)
+            half = res[:, c : c + 512]
+            if eng == 0:
+                nc.vector.tensor_tensor(out=half, in0=s2_banks[h, n, m][:], in1=vbias[:, 512 * n : 512 * n + 512], op=ADD)
+            else:
+                nc.scalar.copy(out=half, in_=s2_banks[h, n, m][:])
+                nc.gpsimd.tensor_tensor(out=half, in0=half, in1=vbias[:, 512 * n : 512 * n + 512], op=ADD)
+            if (h, m) == (1, 3) and n >= 2:
+                nc.sync.dma_start(out=outs[h][128 * m : 128 * m + 128, 512 * n : 512 * (n + 1)], in_=half)
+            elif n % 2 == 1:
+                nc.sync.dma_start(
+                    out=outs[h][128 * m : 128 * m + 128, 512 * (n - 1) : 512 * (n + 1)], in_=res[:]
+                )
 
         T4 = range(4)
-        DVE, ACT, POOL = 0, 1, 2
-        x_transpose(0)
-        x_copy(0)
-        x_transpose(1)
-        x_quant(0)
-        x_copy(1)
-        for t in T4:
-            perm_scales(0, t, nc.vector)
-        perm_words(0, 0, 0, nc.vector)
-        x_transpose(2)
-        x_quant(1)
-        x_copy(2)
-        x_quant(2)
-        s1(0, 0, 0, T4)
-        x_transpose(3)
+        DVE, ACT = 0, 1
+        for g in range(4):
+            for rp in range(2):
+                x_transpose(g, rp)
+                x_copy(g, rp, (ACT, DVE)[rp])
+            if g == 1:
+                perm_scales(0)
+            if g == 2:
+                perm_words(0, 0, 0, 1)
+            if g == 3:
+                perm_words(0, 0, 1, 1)
+            x_quant(g)
+        perm_words(0, 0, 2, 2)
         nc.vector.tensor_copy(out=brow32[0:16, :], in_=brow[0:16, :])
+        for g in range(2):
+            s1(0, 0, g, T4)
         bias_bank = bank("bias_bank")
         nc.tensor.transpose(bias_bank[:, 0:128], brow32[:], ident[:])
-        perm_words(0, 0, 1, nc.vector)
-        x_copy(3)
         nc.scalar.copy(out=bcol[:], in_=bias_bank[:, 0:8])
         nc.scalar.copy(out=bcol2[:], in_=bias_bank[:, 8:16])
-        perm_words(0, 0, 2, nc.vector)
-        x_quant(3)
-        perm_words(0, 0, 3, nc.vector)
-        s1(0, 0, 1, T4)
-        s1(0, 0, 2, T4)
-        s1(0, 0, 3, T4)
-        for g in range(4):
-            perm_words(0, 1, g, nc.vector)
-        perm_table(0, 0, 0, ACT)
-        perm_table(0, 1, 0, DVE)
-        perm_table(0, 0, 1, ACT)
-        perm_table(0, 1, 1, DVE)
+        for g in range(2, 4):
+            s1(0, 0, g, T4)
+        perm_words(0, 1, 0, 4)
+        for half in range(2):
+            perm_table(0, 0, half, DVE)
+            perm_table(0, 1, half, ACT)
+        perm_scales(1)
+        perm_words(1, 0, 0, 4)
+        for t in T4:
+            relu(0, 0, t)
         for t in T4:
             for g in range(4):
                 s1(0, 1, g, [t])
-            relu(0, 0, t)
-        for t in T4:
-            perm_scales(1, t, nc.vector)
-        for g in range(4):
-            perm_words(1, 0, g, nc.vector)
-        perm_table(1, 0, 0, POOL)
-        perm_table(1, 1, 0, ACT)
-        perm_table(1, 0, 1, POOL)
-        perm_table(1, 1, 1, DVE)
-        t_transpose(0, 0)
-        t_transpose(0, 1)
+            relu(0, 1, t)
+        perm_table(1, 0, 0, DVE)
+        perm_table(1, 1, 0, DVE)
         for half in range(2):
             h_inter(0, 0, half, DVE)
+        t_transpose(0, 0)
+        t_transpose(0, 1)
         for rp in range(2):
             for e in range(2):
                 t_copy(0, rp, e, ACT)
+        perm_table(1, 0, 1, DVE)
+        perm_table(1, 1, 1, ACT)
         for half in range(2):
             h_quant(0, 0, half)
-        for t in T4:
-            relu(0, 1, t)
-        for e in range(2):
-            t_quant(0, e)
         for g in range(4):
             s1(1, 0, g, T4)
-        for g in range(4):
-            perm_words(1, 1, g, nc.vector)
-        perm_table(2, 0, 0, DVE)
-        perm_table(2, 1, 0, DVE)
-        t_transpose(1, 0)
-        t_transpose(1, 1)
+        perm_words(1, 1, 0, 4)
         for half in range(2):
             h_inter(0, 1, half, DVE)
+        for e in range(2):
+            t_quant(0, e)
+        for half in range(2):
+            h_quant(0, 1, half)
+        perm_table(2, 0, 0, DVE)
+        perm_table(2, 1, 0, DVE)
+        for t in T4:
+            relu(1, 0, t)
+        t_transpose(1, 0)
+        t_transpose(1, 1)
         for rp in range(2):
             for e in range(2):
                 t_copy(1, rp, e, ACT)
-        for half in range(2):
-            h_quant(0, 1, half)
         perm_table(2, 0, 1, DVE)
         perm_table(2, 1, 1, DVE)
-        for t in T4:
-            relu(1, 0, t)
         for e in range(2):
             t_quant(1, e)
-        perm_table(3, 0, 0, POOL)
-        perm_table(3, 1, 0, POOL)
-        perm_table(3, 0, 1, POOL)
-        for i in range(8):
-            n, m = divmod(i, 4)
-            t, half = divmod(i, 2)
-            s1(1, 1, 2 * half, [t])
-            s1(1, 1, 2 * half + 1, [t])
-            s2(0, n, m)
-            finish(0, n, m)
-            if half == 1 and t > 0:
-                relu(1, 1, t - 1)
-            if i == 0:
-                h_inter(1, 0, 0, ACT)
-            if i == 1:
-                h_inter(1, 0, 1, DVE)
-            if i == 3:
-                h_quant(1, 0, 0)
-                h_quant(1, 0, 1)
-                t_transpose(2, 0)
-                t_transpose(2, 1)
-                for rp in range(2):
-                    for e in range(2):
-                        t_copy(2, rp, e, ACT)
-            if i == 4:
-                perm_table(3, 1, 1, ACT)
-            if i == 7:
-                t_quant(2, 0)
-                t_quant(2, 1)
-        relu(1, 1, 3)
+        for t in range(2):
+            for g in range(4):
+                s1(1, 1, g, [t])
+            relu(1, 1, t)
+        h_inter(1, 0, 0, DVE)
+        h_inter(1, 0, 1, ACT)
+        t_transpose(2, 0)
+        t_transpose(2, 1)
+        perm_table(3, 0, 0, DVE)
+        perm_table(3, 1, 0, ACT)
+        for rp in range(2):
+            for e in range(2):
+                t_copy(2, rp, e, ACT)
+        for t in range(2, 4):
+            for g in range(4):
+                s1(1, 1, g, [t])
+            relu(1, 1, t)
+            for n in range(2):
+                s2(0, n, t - 2)
+                finish(0, n, t - 2)
+        for half in range(2):
+            h_quant(1, 0, half)
+        perm_table(3, 0, 1, DVE)
+        h_inter(1, 1, 0, DVE)
+        perm_table(3, 1, 1, ACT)
+        for n in range(2):
+            s2(0, n, 2)
+            finish(0, n, 2)
+        t_quant(2, 0)
+        t_quant(2, 1)
         t_transpose(3, 0)
         t_transpose(3, 1)
-        h_inter(1, 1, 0, DVE)
+        h_inter(1, 1, 1, ACT)
+        h_quant(1, 1, 0)
+        for n in range(2):
+            s2(0, n, 3)
+            finish(0, n, 3)
+        h_quant(1, 1, 1)
         for rp in range(2):
             for e in range(2):
                 t_copy(3, rp, e, ACT)
         for m in range(4):
-            s2(0, 2, m)
-            finish(0, 2, m)
-            if m == 2:
-                t_quant(3, 0)
-                t_quant(3, 1)
-        h_inter(1, 1, 1, ACT)
-        for half in range(2):
-            h_quant(1, 1, half)
-        for m in range(4):
-            s2(0, 3, m)
-            finish(0, 3, m)
-        for n in range(4):
-            for m in range(4):
+            for n in range(2):
                 s2(1, n, m)
                 finish(1, n, m)
+            if m == 1:
+                t_quant(3, 0)
+                t_quant(3, 1)
+        for h in range(2):
+            for m in range(4):
+                for n in range(2, 4):
+                    s2(h, n, m)
+                    finish(h, n, m, 1 if n == 3 and m < 3 else 0)

@@ -15,7 +15,7 @@ E4M3 = mybir.dt.float8_e4m3fn_x4
 E5M2 = mybir.dt.float8_e5m2_x4
 E2M1 = mybir.dt.float4_e2m1fn_x4
 ADD = mybir.AluOpType.add
-MULT = mybir.AluOpType.mult
+MAX = mybir.AluOpType.max
 RELU = mybir.ActivationFunctionType.Relu
 
 P = 128
@@ -23,6 +23,7 @@ XG = D // 512
 EG = E // 512
 VN = V // 512
 MT = M // 128
+LAST = (1, 1, 3)
 
 
 def tile_tied_vocabulary_head_s9_kernel(
@@ -41,7 +42,7 @@ def tile_tied_vocabulary_head_s9_kernel(
         ctx.enter_context(tc.manual_schedule())
 
         ident = keep.tile([P, P], F32, align_bytes=64)
-        x_raw = keep.tile([P, XG, MT, 512], BF16, align_bytes=64)
+        x_grouped = keep.tile([P, XG, 4 * M], BF16, align_bytes=64)
         x_codes = keep.tile([P, XG, M], U32, align_bytes=64)
         x_planes = keep.tile([P, XG, M], U8, align_bytes=64)
         w_raw = keep.tile([P, 2, XG, 2 * E], U8, align_bytes=64)
@@ -60,11 +61,12 @@ def tile_tied_vocabulary_head_s9_kernel(
         warm = keep.tile([P, 1], F32, align_bytes=64)
         bcols = (bcol, bcol2)
 
-        def load_x(g, r0, n):
-            nc.sync.dma_start(
-                out=x_raw[:, g, r0 : r0 + n, :],
-                in_=x[P * r0 : P * (r0 + n), 512 * g : 512 * g + 512].rearrange("(r p) k -> p r k", p=P),
-            )
+        x_raw = {}
+
+        def load_x(r, k0, n):
+            if k0 == 0:
+                x_raw[r] = flow.tile([P, D], BF16, name="x_raw", tag="rows", bufs=6, align_bytes=64)
+            nc.sync.dma_start(out=x_raw[r][:, k0 : k0 + n], in_=x[P * r : P * r + P, k0 : k0 + n])
 
         def load_words(h, g0, n):
             nc.sync.dma_start(
@@ -83,7 +85,7 @@ def tile_tied_vocabulary_head_s9_kernel(
 
         def load_table(n):
             raw = flow.tile([P, 4, E], BF16, name="t_raw", bufs=4, align_bytes=64)
-            nc.sync.dma_start(out=raw[:], in_=table[512 * n : 512 * n + 512, :].rearrange("(r p) k -> p r k", p=P))
+            nc.sync.dma_start(out=raw[:], in_=table[512 * n : 512 * n + 512, :].rearrange("(p r) k -> p r k", r=4))
             t_raw[n] = raw
 
         nc.vector.memset(warm[:], 0.0)
@@ -92,43 +94,43 @@ def tile_tied_vocabulary_head_s9_kernel(
         make_identity(nc, ident[:])
         nc.vector.memset(brow32[:], 0.0)
         nc.vector.memset(s_raw[:, 1, :, :].rearrange("p g n -> p (g n)").bitcast(I32), 0)
-        load_x(0, 0, 2)
-        load_x(0, 2, 2)
-        load_x(1, 0, 4)
+        load_x(0, 0, 1024)
+        load_x(0, 1024, 1024)
+        load_x(1, 0, 2048)
         load_scales(0)
-        load_x(2, 0, 4)
-        load_x(3, 0, 2)
-        load_x(3, 2, 2)
+        load_x(2, 0, 2048)
+        load_x(3, 0, 1024)
+        load_x(3, 1024, 1024)
         load_words(0, 0, 1)
         load_words(0, 1, 1)
         load_words(0, 2, 2)
-        load_table(0)
-        load_scales(1)
-        load_words(1, 0, 4)
-        load_table(1)
-        load_table(2)
-        nc.sync.dma_start(out=vbias[:], in_=vocab_bias.partition_broadcast(P))
-        load_table(3)
         for h in range(2):
             for e in range(EG):
                 row = 8 * h + 4 * e
-                nc.gpsimd.dma_start(
-                    out=brow[row : row + 4, :].rearrange("t (b i) -> t b i", i=8),
-                    in_=biases[h][512 * e : 512 * e + 512].rearrange("(b t i) -> t b i", t=4, i=8),
+                nc.sync.dma_start(
+                    out=brow[row : row + 4, :].rearrange("t (a i) -> t a i", i=4),
+                    in_=biases[h][512 * e : 512 * e + 512].rearrange("(a t i) -> t a i", t=4, i=4),
                 )
+        load_table(0)
+        load_scales(1)
+        load_table(1)
+        load_words(1, 0, 4)
+        load_table(2)
+        load_table(3)
+        nc.sync.dma_start(out=vbias[:], in_=vocab_bias.partition_broadcast(P))
 
         def perm_words(h, e, g, n):
             nc.vector.tensor_copy(
-                out=w_codes[:, h, g : g + n, 1024 * e : 1024 * e + 1024].bitcast(I32).rearrange("p g (t b w) -> p g t b w", t=4, b=16),
-                in_=w_raw[:, h, g : g + n, 1024 * e : 1024 * e + 1024].bitcast(I32).rearrange("p g (b t w) -> p g t b w", t=4, b=16),
+                out=w_codes[:, h, g : g + n, 1024 * e : 1024 * e + 1024].bitcast(I32).rearrange("p g (t a w) -> p g t a w", t=4, w=2),
+                in_=w_raw[:, h, g : g + n, 1024 * e : 1024 * e + 1024].bitcast(I32).rearrange("p g (a t w) -> p g t a w", t=4, w=2),
             )
 
         def perm_scales(h):
             src = s_raw[:, h, :, :].rearrange("p g n -> p (g n)").bitcast(I32)
             dst = s_planes[:, h, :, :].rearrange("p g n -> p (g n)").bitcast(I32)
             nc.vector.tensor_copy(
-                out=dst.rearrange("p (c t b w) -> p c t b w", t=4, b=16, w=2),
-                in_=src.rearrange("p (c b t w) -> p c t b w", t=4, b=16, w=2),
+                out=dst.rearrange("p (c t a) -> p c t a", t=4, a=32),
+                in_=src.rearrange("p (c a t) -> p c t a", t=4, a=32),
             )
 
         def bank(name):
@@ -136,31 +138,27 @@ def tile_tied_vocabulary_head_s9_kernel(
 
         x_banks = {}
 
-        def x_transpose(g, rp):
-            w = x_raw[:, g, :, :].rearrange("p r k -> p (r k)").bitcast(F32)
+        def x_transpose(r, gp):
+            w = x_raw[r][:].bitcast(F32)
             b = bank("x_bank")
-            for r in range(2):
+            for g in range(2):
                 for u in range(2):
-                    o = 256 * (2 * rp + r)
+                    o = 256 * (2 * gp + g)
                     nc.tensor.transpose(
-                        b[:, 128 * (2 * r + u) : 128 * (2 * r + u) + 128], w[:, o + u : o + 256 : 2], ident[:]
+                        b[:, 128 * (2 * g + u) : 128 * (2 * g + u) + 128], w[:, o + u : o + 256 : 2], ident[:]
                     )
-            x_banks[g, rp] = b
+            x_banks[r, gp] = b
 
-        x_grouped = {}
-
-        def x_copy(g, rp, eng):
-            if rp == 0:
-                x_grouped[g] = flow.tile([P, 2048], BF16, name="x_grouped", bufs=3, align_bytes=64)
-            dst = x_grouped[g][:, 1024 * rp : 1024 * rp + 1024].bitcast(F32).rearrange("p (r n u) -> p r n u", r=2, u=2)
-            src = x_banks[g, rp][:].rearrange("p (r u n) -> p r n u", r=2, u=2)
+        def x_copy(r, gp, eng):
+            dst = x_grouped[:, 2 * gp : 2 * gp + 2, 512 * r : 512 * r + 512].bitcast(F32).rearrange("p g (n u) -> p g n u", u=2)
+            src = x_banks[r, gp][:].rearrange("p (g u n) -> p g n u", g=2, u=2)
             if eng == 0:
                 nc.vector.tensor_copy(out=dst, in_=src)
             else:
                 nc.scalar.copy(out=dst, in_=src)
 
         def x_quant(g):
-            nc.vector.quantize_mx(out=x_codes[:, g, :].bitcast(E4M3), scales=x_planes[:, g, :], in_=x_grouped[g][:])
+            nc.vector.quantize_mx(out=x_codes[:, g, :].bitcast(E4M3), scales=x_planes[:, g, :], in_=x_grouped[:, g, :])
 
         s1_banks = {}
 
@@ -181,17 +179,19 @@ def tile_tied_vocabulary_head_s9_kernel(
 
         planes = {}
 
-        def relu(h, e, t):
-            if t == 0:
+        def relu(h, e, t, eng):
+            if (h, e) not in planes:
                 planes[h, e] = flow.tile([P, 4, M], BF16, name="planes", bufs=2, align_bytes=64)
-            nc.scalar.activation(
-                out=planes[h, e][:, t, :], in_=s1_banks[h, e, t][:], func=RELU, bias=bcols[h][:, 4 * e + t : 4 * e + t + 1]
-            )
+            dst, src, b = planes[h, e][:, t, :], s1_banks[h, e, t][:], bcols[h][:, 4 * e + t : 4 * e + t + 1]
+            if eng == 0:
+                nc.vector.tensor_scalar(out=dst, in0=src, scalar1=b, scalar2=0.0, op0=ADD, op1=MAX)
+            else:
+                nc.scalar.activation(out=dst, in_=src, func=RELU, bias=b)
 
         grouped_h = {}
 
         def h_inter(h, e, half, eng):
-            if half == 0:
+            if (h, e) not in grouped_h:
                 grouped_h[h, e] = flow.tile([P, M, 4], BF16, name="h_grouped", bufs=2, align_bytes=64)
             a = 256 * half
             dst = grouped_h[h, e][:, a : a + 256, :]
@@ -212,18 +212,16 @@ def tile_tied_vocabulary_head_s9_kernel(
         t_perm = {}
 
         def perm_table(n, u, half, eng):
-            if (u, half) == (0, 0):
+            if n not in t_perm:
                 t_perm[n] = flow.tile([P, 2, 2048], BF16, name="t_perm", bufs=3, align_bytes=64)
-            src = t_raw[n][:].rearrange("p r k -> p (r k)").rearrange("p (c u e i) -> p c u i e", u=2, e=2, i=8)
-            dst = t_perm[n][:].rearrange("p u (c i e) -> p c u i e", i=8, e=2)
-            dst = dst[:, 64 * half : 64 * half + 64, u]
-            src = src[:, 64 * half : 64 * half + 64, u]
+            src = t_raw[n][:].rearrange("p r k -> p (r k)").rearrange("p (c u e i) -> p c u i e", u=2, e=2, i=4)
+            dst = t_perm[n][:].rearrange("p u (c i e) -> p c u i e", i=4, e=2)
+            dst = dst[:, 128 * half : 128 * half + 128, u]
+            src = src[:, 128 * half : 128 * half + 128, u]
             if eng == 0:
                 nc.vector.tensor_copy(out=dst, in_=src)
-            elif eng == 1:
-                nc.scalar.copy(out=dst, in_=src)
             else:
-                nc.gpsimd.tensor_scalar(out=dst, in0=src, scalar1=1.0, scalar2=0.0, op0=MULT, op1=ADD)
+                nc.scalar.copy(out=dst, in_=src)
 
         t_banks = {}
 
@@ -243,10 +241,10 @@ def tile_tied_vocabulary_head_s9_kernel(
         t_grouped = {}
 
         def t_copy(n, rp, e, eng):
-            if rp == 0:
-                t_grouped[n, e] = flow.tile([P, 2048], BF16, name="t_grouped", bufs=4, align_bytes=64)
-            dst = t_grouped[n, e][:, 1024 * rp : 1024 * rp + 1024].bitcast(F32).rearrange("p (r n u) -> p r n u", r=2, u=2)
-            src = t_banks[n, e, rp][:].rearrange("p (r u n) -> p r n u", r=2, u=2)
+            if (n, e) not in t_grouped:
+                t_grouped[n, e] = flow.tile([P, 2048], BF16, name="t_grouped", tag="rows", bufs=6, align_bytes=64)
+            dst = t_grouped[n, e][:].bitcast(F32).rearrange("p (q r u) -> p q r u", r=4, u=2)[:, :, 2 * rp : 2 * rp + 2]
+            src = t_banks[n, e, rp][:].rearrange("p (r u q) -> p q r u", r=2, u=2)
             if eng == 0:
                 nc.vector.tensor_copy(out=dst, in_=src)
             else:
@@ -276,143 +274,252 @@ def tile_tied_vocabulary_head_s9_kernel(
         res_tiles = {}
 
         def finish(h, n, m, eng=0):
-            if n % 2 == 0:
-                res_tiles[h, n, m] = flow.tile([P, 1024], F32, name="res", bufs=6, align_bytes=64)
-            res = res_tiles[h, n - n % 2, m]
-            c = 512 * (n % 2)
-            half = res[:, c : c + 512]
+            pair = (h, n // 2, m)
+            second = pair in res_tiles
+            if not second:
+                res_tiles[pair] = flow.tile([P, 1024], F32, name="res", bufs=6, align_bytes=64)
+            res = res_tiles[pair]
+            half = res[:, 512 * (n % 2) : 512 * (n % 2) + 512]
             if eng == 0:
                 nc.vector.tensor_tensor(out=half, in0=s2_banks[h, n, m][:], in1=vbias[:, 512 * n : 512 * n + 512], op=ADD)
             else:
                 nc.scalar.copy(out=half, in_=s2_banks[h, n, m][:])
                 nc.gpsimd.tensor_tensor(out=half, in0=half, in1=vbias[:, 512 * n : 512 * n + 512], op=ADD)
-            if (h, m) == (1, 3) and n >= 2:
-                nc.sync.dma_start(out=outs[h][128 * m : 128 * m + 128, 512 * n : 512 * (n + 1)], in_=half)
-            elif n % 2 == 1:
-                nc.sync.dma_start(
-                    out=outs[h][128 * m : 128 * m + 128, 512 * (n - 1) : 512 * (n + 1)], in_=res[:]
-                )
+            rows = outs[h][128 * m : 128 * m + 128, :]
+            if pair == LAST:
+                nc.sync.dma_start(out=rows[:, 512 * n : 512 * (n + 1)], in_=half)
+            elif second:
+                nc.sync.dma_start(out=rows[:, 1024 * (n // 2) : 1024 * (n // 2) + 1024], in_=res[:])
 
-        T4 = range(4)
         DVE, ACT = 0, 1
-        for g in range(4):
-            for rp in range(2):
-                x_transpose(g, rp)
-                x_copy(g, rp, (ACT, DVE)[rp])
-            if g == 1:
+        for r in range(4):
+            for gp in range(2):
+                x_transpose(r, gp)
+                x_copy(r, gp, DVE if (r, gp) == (3, 0) else ACT)
+            if r == 1:
                 perm_scales(0)
-            if g == 2:
-                perm_words(0, 0, 0, 1)
-            if g == 3:
-                perm_words(0, 0, 1, 1)
-            x_quant(g)
-        perm_words(0, 0, 2, 2)
-        nc.vector.tensor_copy(out=brow32[0:16, :], in_=brow[0:16, :])
-        for g in range(2):
-            s1(0, 0, g, T4)
+        perm_words(0, 0, 0, 1)
+        x_quant(0)
+        x_quant(1)
+        perm_words(0, 0, 1, 1)
+        x_quant(2)
+        nc.scalar.copy(out=brow32[0:16, :], in_=brow[0:16, :])
+        perm_words(0, 0, 2, 1)
+        x_quant(3)
+        s1(0, 0, 0, [0])
+        s1(0, 0, 0, [1])
+        s1(0, 0, 0, [2])
+        s1(0, 0, 0, [3])
+        s1(0, 0, 1, [0])
+        s1(0, 0, 1, [1])
+        s1(0, 0, 1, [2])
+        s1(0, 0, 1, [3])
+        perm_words(0, 1, 0, 4)
         bias_bank = bank("bias_bank")
         nc.tensor.transpose(bias_bank[:, 0:128], brow32[:], ident[:])
         nc.scalar.copy(out=bcol[:], in_=bias_bank[:, 0:8])
-        nc.scalar.copy(out=bcol2[:], in_=bias_bank[:, 8:16])
-        for g in range(2, 4):
-            s1(0, 0, g, T4)
-        perm_words(0, 1, 0, 4)
-        for half in range(2):
-            perm_table(0, 0, half, DVE)
-            perm_table(0, 1, half, ACT)
-        perm_scales(1)
-        perm_words(1, 0, 0, 4)
-        for t in T4:
-            relu(0, 0, t)
-        for t in T4:
-            for g in range(4):
-                s1(0, 1, g, [t])
-            relu(0, 1, t)
-        perm_table(1, 0, 0, DVE)
-        perm_table(1, 1, 0, DVE)
-        for half in range(2):
-            h_inter(0, 0, half, DVE)
-        t_transpose(0, 0)
+        s1(0, 0, 2, [0])
+        s1(0, 0, 2, [1])
+        s1(0, 0, 2, [2])
+        s1(0, 0, 2, [3])
+        perm_words(0, 0, 3, 1)
+        perm_table(0, 1, 0, DVE)
+        s1(0, 0, 3, [0])
+        s1(0, 0, 3, [1])
+        s1(0, 0, 3, [2])
+        s1(0, 0, 3, [3])
+        perm_table(0, 0, 1, ACT)
+        relu(0, 0, 0, ACT)
+        relu(0, 0, 3, ACT)
+        perm_table(0, 1, 1, DVE)
+        perm_table(0, 0, 0, DVE)
+        s1(0, 1, 0, [0])
+        s1(0, 1, 1, [0])
+        s1(0, 1, 2, [0])
+        s1(0, 1, 3, [0])
         t_transpose(0, 1)
-        for rp in range(2):
-            for e in range(2):
-                t_copy(0, rp, e, ACT)
-        perm_table(1, 0, 1, DVE)
+        relu(0, 0, 1, ACT)
+        relu(0, 0, 2, DVE)
+        perm_scales(1)
+        s1(0, 1, 0, [1])
+        s1(0, 1, 1, [1])
+        s1(0, 1, 2, [1])
+        s1(0, 1, 3, [1])
+        perm_table(1, 0, 0, DVE)
+        relu(0, 1, 0, ACT)
+        s1(0, 1, 0, [3])
+        s1(0, 1, 1, [3])
+        s1(0, 1, 2, [3])
+        s1(0, 1, 3, [3])
         perm_table(1, 1, 1, ACT)
-        for half in range(2):
-            h_quant(0, 0, half)
-        for g in range(4):
-            s1(1, 0, g, T4)
-        perm_words(1, 1, 0, 4)
-        for half in range(2):
-            h_inter(0, 1, half, DVE)
-        for e in range(2):
-            t_quant(0, e)
-        for half in range(2):
-            h_quant(0, 1, half)
-        perm_table(2, 0, 0, DVE)
-        perm_table(2, 1, 0, DVE)
-        for t in T4:
-            relu(1, 0, t)
-        t_transpose(1, 0)
+        perm_table(1, 0, 1, DVE)
+        h_inter(0, 0, 1, DVE)
+        s1(0, 1, 0, [2])
+        s1(0, 1, 1, [2])
+        s1(0, 1, 2, [2])
+        s1(0, 1, 3, [2])
         t_transpose(1, 1)
-        for rp in range(2):
-            for e in range(2):
-                t_copy(1, rp, e, ACT)
-        perm_table(2, 0, 1, DVE)
+        t_copy(0, 1, 0, ACT)
+        t_copy(0, 1, 1, ACT)
+        perm_table(1, 1, 0, DVE)
+        perm_words(1, 1, 0, 4)
+        nc.scalar.copy(out=bcol2[:], in_=bias_bank[:, 8:16])
+        perm_words(1, 0, 0, 4)
+        relu(0, 1, 3, ACT)
+        relu(0, 1, 1, ACT)
+        h_inter(0, 0, 0, DVE)
+        t_transpose(1, 0)
+        relu(0, 1, 2, ACT)
+        t_copy(1, 1, 1, ACT)
+        perm_table(2, 1, 0, DVE)
+        perm_table(2, 0, 0, DVE)
+        t_transpose(0, 0)
         perm_table(2, 1, 1, DVE)
-        for e in range(2):
-            t_quant(1, e)
-        for t in range(2):
-            for g in range(4):
-                s1(1, 1, g, [t])
-            relu(1, 1, t)
-        h_inter(1, 0, 0, DVE)
-        h_inter(1, 0, 1, ACT)
-        t_transpose(2, 0)
+        t_copy(1, 0, 0, ACT)
+        t_copy(1, 1, 0, ACT)
+        s1(1, 1, 0, [1])
+        s1(1, 1, 1, [1])
+        s1(1, 1, 2, [1])
+        s1(1, 1, 3, [1])
+        t_copy(0, 0, 1, ACT)
+        perm_table(2, 0, 1, ACT)
+        h_quant(0, 0, 0)
+        s1(1, 0, 0, [0])
+        s1(1, 0, 0, [1])
+        s1(1, 0, 0, [2])
+        s1(1, 0, 0, [3])
+        s1(1, 0, 1, [0])
+        s1(1, 0, 1, [1])
+        s1(1, 0, 1, [2])
+        s1(1, 0, 1, [3])
+        t_copy(0, 0, 0, ACT)
+        t_copy(1, 0, 1, ACT)
+        t_quant(0, 1)
+        h_inter(0, 1, 0, DVE)
+        h_inter(0, 1, 1, DVE)
+        h_quant(0, 1, 0)
+        h_quant(0, 0, 1)
+        s1(1, 0, 2, [0])
+        s1(1, 0, 2, [1])
+        s1(1, 0, 2, [2])
+        s1(1, 0, 2, [3])
+        s1(1, 0, 3, [0])
+        s1(1, 0, 3, [1])
+        s1(1, 0, 3, [2])
+        s1(1, 0, 3, [3])
+        t_quant(0, 0)
+        perm_table(3, 0, 0, ACT)
         t_transpose(2, 1)
-        perm_table(3, 0, 0, DVE)
+        relu(1, 0, 2, ACT)
+        relu(1, 0, 0, ACT)
+        t_transpose(2, 0)
+        t_quant(1, 1)
+        s2(0, 0, 1)
+        relu(1, 0, 1, ACT)
         perm_table(3, 1, 0, ACT)
-        for rp in range(2):
-            for e in range(2):
-                t_copy(2, rp, e, ACT)
-        for t in range(2, 4):
-            for g in range(4):
-                s1(1, 1, g, [t])
-            relu(1, 1, t)
-            for n in range(2):
-                s2(0, n, t - 2)
-                finish(0, n, t - 2)
-        for half in range(2):
-            h_quant(1, 0, half)
+        relu(1, 0, 3, ACT)
+        h_quant(0, 1, 1)
+        t_copy(2, 1, 1, DVE)
+        t_quant(1, 0)
+        s1(1, 1, 0, [0])
+        s1(1, 1, 1, [0])
+        s1(1, 1, 2, [0])
+        s1(1, 1, 3, [0])
         perm_table(3, 0, 1, DVE)
-        h_inter(1, 1, 0, DVE)
-        perm_table(3, 1, 1, ACT)
-        for n in range(2):
-            s2(0, n, 2)
-            finish(0, n, 2)
-        t_quant(2, 0)
-        t_quant(2, 1)
-        t_transpose(3, 0)
+        finish(0, 0, 1, DVE)
+        s2(0, 1, 0)
+        s2(0, 1, 1)
+        perm_table(3, 1, 1, DVE)
+        relu(1, 1, 0, ACT)
+        finish(0, 1, 0, DVE)
+        s2(0, 0, 0)
+        finish(0, 0, 0, DVE)
         t_transpose(3, 1)
-        h_inter(1, 1, 1, ACT)
+        t_copy(2, 1, 0, ACT)
+        t_transpose(3, 0)
+        relu(1, 1, 1, ACT)
+        t_copy(2, 0, 1, ACT)
+        t_copy(2, 0, 0, ACT)
+        t_copy(3, 1, 1, ACT)
+        s2(0, 1, 2)
+        s2(0, 0, 3)
+        finish(0, 1, 1, DVE)
+        t_quant(2, 1)
+        t_copy(3, 0, 1, ACT)
+        s1(1, 1, 0, [3])
+        s1(1, 1, 1, [3])
+        s1(1, 1, 2, [3])
+        s1(1, 1, 3, [3])
+        t_quant(2, 0)
+        finish(0, 1, 2, DVE)
+        finish(0, 0, 3, DVE)
+        t_copy(3, 0, 0, ACT)
+        s2(0, 1, 3)
+        s2(0, 0, 2)
+        t_copy(3, 1, 0, ACT)
+        h_inter(1, 0, 0, ACT)
+        t_quant(3, 1)
+        s1(1, 1, 0, [2])
+        s1(1, 1, 1, [2])
+        s1(1, 1, 2, [2])
+        s1(1, 1, 3, [2])
+        t_quant(3, 0)
+        s2(0, 2, 0)
+        s2(0, 3, 0)
+        relu(1, 1, 3, ACT)
+        finish(0, 0, 2, DVE)
+        relu(1, 1, 2, ACT)
+        h_quant(1, 0, 0)
+        s2(0, 3, 2)
+        s2(0, 2, 2)
+        s2(0, 3, 1)
+        finish(0, 1, 3, DVE)
+        finish(0, 2, 0, DVE)
+        finish(0, 3, 0, DVE)
+        h_inter(1, 1, 0, ACT)
+        finish(0, 3, 2, DVE)
         h_quant(1, 1, 0)
-        for n in range(2):
-            s2(0, n, 3)
-            finish(0, n, 3)
+        h_inter(1, 1, 1, ACT)
+        s2(0, 2, 1)
+        s2(1, 1, 0)
+        finish(0, 2, 2, DVE)
+        s2(0, 2, 3)
+        s2(1, 0, 0)
+        finish(0, 2, 1, DVE)
+        s2(0, 3, 3)
+        finish(0, 3, 1, DVE)
+        s2(1, 1, 1)
+        s2(1, 0, 1)
+        finish(0, 2, 3, DVE)
+        finish(1, 1, 0, ACT)
+        finish(1, 0, 0, DVE)
+        h_inter(1, 0, 1, ACT)
+        h_quant(1, 0, 1)
+        finish(0, 3, 3, DVE)
+        s2(1, 3, 0)
         h_quant(1, 1, 1)
-        for rp in range(2):
-            for e in range(2):
-                t_copy(3, rp, e, ACT)
-        for m in range(4):
-            for n in range(2):
-                s2(1, n, m)
-                finish(1, n, m)
-            if m == 1:
-                t_quant(3, 0)
-                t_quant(3, 1)
-        for h in range(2):
-            for m in range(4):
-                for n in range(2, 4):
-                    s2(h, n, m)
-                    finish(h, n, m, 1 if n == 3 and m < 3 else 0)
+        s2(1, 3, 1)
+        finish(1, 1, 1, ACT)
+        finish(1, 0, 1, DVE)
+        s2(1, 2, 0)
+        finish(1, 3, 0, ACT)
+        s2(1, 1, 2)
+        s2(1, 2, 1)
+        s2(1, 2, 2)
+        s2(1, 2, 3)
+        s2(1, 0, 2)
+        finish(1, 2, 0, DVE)
+        s2(1, 1, 3)
+        finish(1, 2, 1, DVE)
+        finish(1, 2, 3, DVE)
+        finish(1, 2, 2, DVE)
+        s2(1, 3, 2)
+        s2(1, 0, 3)
+        finish(1, 3, 1, ACT)
+        s2(1, 3, 3)
+        finish(1, 1, 2, ACT)
+        finish(1, 0, 2, DVE)
+        finish(1, 1, 3, DVE)
+        finish(1, 0, 3, DVE)
+        finish(1, 3, 2, ACT)
+        finish(1, 3, 3, DVE)

from contextlib import ExitStack

import concourse.mybir as mybir
from concourse.masks import make_identity

M, D, E, V = 512, 2048, 1024, 2048
FLOPS = 2 * 2 * M * D * E + 2 * 2 * M * E * V

F32 = mybir.dt.float32
BF16 = mybir.dt.bfloat16
I32 = mybir.dt.int32
U32 = mybir.dt.uint32
U8 = mybir.dt.uint8
E4M3 = mybir.dt.float8_e4m3fn_x4
E5M2 = mybir.dt.float8_e5m2_x4
E2M1 = mybir.dt.float4_e2m1fn_x4
ADD = mybir.AluOpType.add
MAX = mybir.AluOpType.max
RELU = mybir.ActivationFunctionType.Relu

P = 128
XG = D // 512
EG = E // 512
VN = V // 512
MT = M // 128
LAST = (1, 1, 3)


def tile_tied_vocabulary_head_s9_kernel(
    tc, x, near_words, near_scales, near_bias, far_words, far_scales, far_bias, table, vocab_bias, out_0, out_1
):
    nc = tc.nc
    words = (near_words, far_words)
    scales = (near_scales, far_scales)
    biases = (near_bias, far_bias)
    outs = (out_0, out_1)

    with ExitStack() as ctx:
        keep = ctx.enter_context(tc.tile_pool(name="keep", bufs=1))
        flow = ctx.enter_context(tc.tile_pool(name="flow", bufs=2))
        psum = ctx.enter_context(tc.psum_pool(name="psum", bufs=8))
        ctx.enter_context(tc.manual_schedule())

        ident = keep.tile([P, P], F32, align_bytes=64)
        x_grouped = keep.tile([P, XG, 4 * M], BF16, align_bytes=64)
        x_codes = keep.tile([P, XG, M], U32, align_bytes=64)
        x_planes = keep.tile([P, XG, M], U8, align_bytes=64)
        w_raw = keep.tile([P, 2, XG, 2 * E], U8, align_bytes=64)
        w_codes = keep.tile([P, 2, XG, 2 * E], U8, align_bytes=64)
        s_raw = keep.tile([P, 2, XG, E], U8, align_bytes=64)
        s_planes = keep.tile([P, 2, XG, E], U8, align_bytes=64)
        t_codes = keep.tile([P, VN, EG, 512], U32, align_bytes=64)
        t_planes = keep.tile([P, VN, EG, 512], U8, align_bytes=64)
        h_codes = keep.tile([P, 2, EG, M], U32, align_bytes=64)
        h_planes = keep.tile([P, 2, EG, M], U8, align_bytes=64)
        vbias = keep.tile([P, V], BF16, align_bytes=64)
        brow = keep.tile([P, P], BF16, align_bytes=64)
        brow32 = keep.tile([P, P], F32, align_bytes=64)
        bcol = keep.tile([P, 4 * EG], F32, align_bytes=64)
        bcol2 = keep.tile([P, 4 * EG], F32, align_bytes=64)
        warm = keep.tile([P, 1], F32, align_bytes=64)
        bcols = (bcol, bcol2)

        x_raw = {}

        def load_x(r, k0, n):
            if k0 == 0:
                x_raw[r] = flow.tile([P, D], BF16, name="x_raw", tag="rows", bufs=6, align_bytes=64)
            nc.sync.dma_start(out=x_raw[r][:, k0 : k0 + n], in_=x[P * r : P * r + P, k0 : k0 + n])

        def load_words(h, g0, n):
            nc.sync.dma_start(
                out=w_raw[:, h, g0 : g0 + n, :].bitcast(I32),
                in_=words[h][g0 : g0 + n].rearrange("g p c -> p g c").bitcast(I32),
            )

        def load_scales(h):
            for q in range(4):
                nc.sync.dma_start(
                    out=s_raw[32 * q : 32 * q + 4, h, :, :].bitcast(I32),
                    in_=scales[h][:, 4 * q : 4 * q + 4, :].rearrange("g r n -> r g n").bitcast(I32),
                )

        t_raw = {}

        def load_table(n):
            raw = flow.tile([P, 4, E], BF16, name="t_raw", bufs=4, align_bytes=64)
            nc.sync.dma_start(out=raw[:], in_=table[512 * n : 512 * n + 512, :].rearrange("(p r) k -> p r k", r=4))
            t_raw[n] = raw

        nc.vector.memset(warm[:], 0.0)
        nc.scalar.activation(out=warm[:], in_=warm[:], func=RELU)
        nc.vector.memset(s_raw[:, 0, :, :].rearrange("p g n -> p (g n)").bitcast(I32), 0)
        make_identity(nc, ident[:])
        nc.vector.memset(brow32[:], 0.0)
        nc.vector.memset(s_raw[:, 1, :, :].rearrange("p g n -> p (g n)").bitcast(I32), 0)
        load_x(0, 0, 1024)
        load_x(0, 1024, 1024)
        load_x(1, 0, 2048)
        load_scales(0)
        load_x(2, 0, 2048)
        load_x(3, 0, 1024)
        load_x(3, 1024, 1024)
        load_words(0, 0, 1)
        load_words(0, 1, 1)
        load_words(0, 2, 2)
        for h in range(2):
            for e in range(EG):
                row = 8 * h + 4 * e
                nc.sync.dma_start(
                    out=brow[row : row + 4, :].rearrange("t (a i) -> t a i", i=4),
                    in_=biases[h][512 * e : 512 * e + 512].rearrange("(a t i) -> t a i", t=4, i=4),
                )
        load_table(0)
        load_scales(1)
        load_table(1)
        load_words(1, 0, 4)
        load_table(2)
        load_table(3)
        nc.sync.dma_start(out=vbias[:], in_=vocab_bias.partition_broadcast(P))

        def perm_words(h, e, g, n):
            nc.vector.tensor_copy(
                out=w_codes[:, h, g : g + n, 1024 * e : 1024 * e + 1024].bitcast(I32).rearrange("p g (t a w) -> p g t a w", t=4, w=2),
                in_=w_raw[:, h, g : g + n, 1024 * e : 1024 * e + 1024].bitcast(I32).rearrange("p g (a t w) -> p g t a w", t=4, w=2),
            )

        def perm_scales(h):
            src = s_raw[:, h, :, :].rearrange("p g n -> p (g n)").bitcast(I32)
            dst = s_planes[:, h, :, :].rearrange("p g n -> p (g n)").bitcast(I32)
            nc.vector.tensor_copy(
                out=dst.rearrange("p (c t a) -> p c t a", t=4, a=32),
                in_=src.rearrange("p (c a t) -> p c t a", t=4, a=32),
            )

        def bank(name):
            return psum.tile([P, 512], F32, name=name, tag="bank", bufs=8)

        x_banks = {}

        def x_transpose(r, gp):
            w = x_raw[r][:].bitcast(F32)
            b = bank("x_bank")
            for g in range(2):
                for u in range(2):
                    o = 256 * (2 * gp + g)
                    nc.tensor.transpose(
                        b[:, 128 * (2 * g + u) : 128 * (2 * g + u) + 128], w[:, o + u : o + 256 : 2], ident[:]
                    )
            x_banks[r, gp] = b

        def x_copy(r, gp, eng):
            dst = x_grouped[:, 2 * gp : 2 * gp + 2, 512 * r : 512 * r + 512].bitcast(F32).rearrange("p g (n u) -> p g n u", u=2)
            src = x_banks[r, gp][:].rearrange("p (g u n) -> p g n u", g=2, u=2)
            if eng == 0:
                nc.vector.tensor_copy(out=dst, in_=src)
            else:
                nc.scalar.copy(out=dst, in_=src)

        def x_quant(g):
            nc.vector.quantize_mx(out=x_codes[:, g, :].bitcast(E4M3), scales=x_planes[:, g, :], in_=x_grouped[:, g, :])

        s1_banks = {}

        def s1(h, e, g, ts):
            for t in ts:
                if g == 0:
                    s1_banks[h, e, t] = bank("s1_bank")
                c = 512 * e + 128 * t
                nc.tensor.matmul_mx(
                    out=s1_banks[h, e, t][:],
                    lhsT=w_codes[:, h, g, 2 * c : 2 * c + 256].bitcast(E2M1),
                    lhsT_scale=s_planes[:, h, g, c : c + 128],
                    rhs=x_codes[:, g, :].bitcast(E4M3),
                    rhs_scale=x_planes[:, g, :],
                    start=(g == 0),
                    stop=(g == XG - 1),
                )

        planes = {}

        def relu(h, e, t, eng):
            if (h, e) not in planes:
                planes[h, e] = flow.tile([P, 4, M], BF16, name="planes", bufs=2, align_bytes=64)
            dst, src, b = planes[h, e][:, t, :], s1_banks[h, e, t][:], bcols[h][:, 4 * e + t : 4 * e + t + 1]
            if eng == 0:
                nc.vector.tensor_scalar(out=dst, in0=src, scalar1=b, scalar2=0.0, op0=ADD, op1=MAX)
            else:
                nc.scalar.activation(out=dst, in_=src, func=RELU, bias=b)

        grouped_h = {}

        def h_inter(h, e, half, eng):
            if (h, e) not in grouped_h:
                grouped_h[h, e] = flow.tile([P, M, 4], BF16, name="h_grouped", bufs=2, align_bytes=64)
            a = 256 * half
            dst = grouped_h[h, e][:, a : a + 256, :]
            src = planes[h, e][:, :, a : a + 256].rearrange("p t n -> p n t")
            if eng == 0:
                nc.vector.tensor_copy(out=dst, in_=src)
            else:
                nc.scalar.copy(out=dst, in_=src)

        def h_quant(h, e, half):
            a = 256 * half
            nc.vector.quantize_mx(
                out=h_codes[:, h, e, a : a + 256].bitcast(E5M2),
                scales=h_planes[:, h, e, a : a + 256],
                in_=grouped_h[h, e][:, a : a + 256, :].rearrange("p n t -> p (n t)"),
            )

        t_perm = {}

        def perm_table(n, u, half, eng):
            if n not in t_perm:
                t_perm[n] = flow.tile([P, 2, 2048], BF16, name="t_perm", bufs=3, align_bytes=64)
            src = t_raw[n][:].rearrange("p r k -> p (r k)").rearrange("p (c u e i) -> p c u i e", u=2, e=2, i=4)
            dst = t_perm[n][:].rearrange("p u (c i e) -> p c u i e", i=4, e=2)
            dst = dst[:, 128 * half : 128 * half + 128, u]
            src = src[:, 128 * half : 128 * half + 128, u]
            if eng == 0:
                nc.vector.tensor_copy(out=dst, in_=src)
            else:
                nc.scalar.copy(out=dst, in_=src)

        t_banks = {}

        def t_transpose(n, rp):
            for e in range(EG):
                b = bank("t_bank")
                for r in range(2):
                    for u in range(2):
                        o = 256 * (2 * rp + r) + 128 * e
                        nc.tensor.transpose(
                            b[:, 128 * (2 * r + u) : 128 * (2 * r + u) + 128],
                            t_perm[n][:, u, :].bitcast(F32)[:, o : o + 128],
                            ident[:],
                        )
                t_banks[n, e, rp] = b

        t_grouped = {}

        def t_copy(n, rp, e, eng):
            if (n, e) not in t_grouped:
                t_grouped[n, e] = flow.tile([P, 2048], BF16, name="t_grouped", tag="rows", bufs=6, align_bytes=64)
            dst = t_grouped[n, e][:].bitcast(F32).rearrange("p (q r u) -> p q r u", r=4, u=2)[:, :, 2 * rp : 2 * rp + 2]
            src = t_banks[n, e, rp][:].rearrange("p (r u q) -> p q r u", r=2, u=2)
            if eng == 0:
                nc.vector.tensor_copy(out=dst, in_=src)
            else:
                nc.scalar.copy(out=dst, in_=src)

        def t_quant(n, e):
            nc.vector.quantize_mx(
                out=t_codes[:, n, e, :].bitcast(E4M3), scales=t_planes[:, n, e, :], in_=t_grouped[n, e][:]
            )

        s2_banks = {}

        def s2(h, n, m):
            b = bank("s2_bank")
            for e in range(EG):
                nc.tensor.matmul_mx(
                    out=b[:],
                    lhsT=h_codes[:, h, e, 128 * m : 128 * m + 128].bitcast(E5M2),
                    lhsT_scale=h_planes[:, h, e, 128 * m : 128 * m + 128],
                    rhs=t_codes[:, n, e, :].bitcast(E4M3),
                    rhs_scale=t_planes[:, n, e, :],
                    start=(e == 0),
                    stop=(e == EG - 1),
                )
            s2_banks[h, n, m] = b

        res_tiles = {}

        def finish(h, n, m, eng=0):
            pair = (h, n // 2, m)
            second = pair in res_tiles
            if not second:
                res_tiles[pair] = flow.tile([P, 1024], F32, name="res", bufs=6, align_bytes=64)
            res = res_tiles[pair]
            half = res[:, 512 * (n % 2) : 512 * (n % 2) + 512]
            if eng == 0:
                nc.vector.tensor_tensor(out=half, in0=s2_banks[h, n, m][:], in1=vbias[:, 512 * n : 512 * n + 512], op=ADD)
            else:
                nc.scalar.copy(out=half, in_=s2_banks[h, n, m][:])
                nc.gpsimd.tensor_tensor(out=half, in0=half, in1=vbias[:, 512 * n : 512 * n + 512], op=ADD)
            rows = outs[h][128 * m : 128 * m + 128, :]
            if pair == LAST:
                nc.sync.dma_start(out=rows[:, 512 * n : 512 * (n + 1)], in_=half)
            elif second:
                nc.sync.dma_start(out=rows[:, 1024 * (n // 2) : 1024 * (n // 2) + 1024], in_=res[:])

        DVE, ACT = 0, 1
        for r in range(4):
            for gp in range(2):
                x_transpose(r, gp)
                x_copy(r, gp, DVE if (r, gp) == (3, 0) else ACT)
            if r == 1:
                perm_scales(0)
        perm_words(0, 0, 0, 1)
        x_quant(0)
        x_quant(1)
        perm_words(0, 0, 1, 1)
        x_quant(2)
        nc.scalar.copy(out=brow32[0:16, :], in_=brow[0:16, :])
        perm_words(0, 0, 2, 1)
        x_quant(3)
        s1(0, 0, 0, [0])
        s1(0, 0, 0, [1])
        s1(0, 0, 0, [2])
        s1(0, 0, 0, [3])
        s1(0, 0, 1, [0])
        s1(0, 0, 1, [1])
        s1(0, 0, 1, [2])
        s1(0, 0, 1, [3])
        perm_words(0, 1, 0, 4)
        bias_bank = bank("bias_bank")
        nc.tensor.transpose(bias_bank[:, 0:128], brow32[:], ident[:])
        nc.scalar.copy(out=bcol[:], in_=bias_bank[:, 0:8])
        s1(0, 0, 2, [0])
        s1(0, 0, 2, [1])
        s1(0, 0, 2, [2])
        s1(0, 0, 2, [3])
        perm_words(0, 0, 3, 1)
        perm_table(0, 1, 0, DVE)
        s1(0, 0, 3, [0])
        s1(0, 0, 3, [1])
        s1(0, 0, 3, [2])
        s1(0, 0, 3, [3])
        perm_table(0, 0, 1, ACT)
        relu(0, 0, 0, ACT)
        relu(0, 0, 3, ACT)
        perm_table(0, 1, 1, DVE)
        perm_table(0, 0, 0, DVE)
        s1(0, 1, 0, [0])
        s1(0, 1, 1, [0])
        s1(0, 1, 2, [0])
        s1(0, 1, 3, [0])
        t_transpose(0, 1)
        relu(0, 0, 1, ACT)
        relu(0, 0, 2, DVE)
        perm_scales(1)
        s1(0, 1, 0, [1])
        s1(0, 1, 1, [1])
        s1(0, 1, 2, [1])
        s1(0, 1, 3, [1])
        perm_table(1, 0, 0, DVE)
        relu(0, 1, 0, ACT)
        s1(0, 1, 0, [3])
        s1(0, 1, 1, [3])
        s1(0, 1, 2, [3])
        s1(0, 1, 3, [3])
        perm_table(1, 1, 1, ACT)
        perm_table(1, 0, 1, DVE)
        h_inter(0, 0, 1, DVE)
        s1(0, 1, 0, [2])
        s1(0, 1, 1, [2])
        s1(0, 1, 2, [2])
        s1(0, 1, 3, [2])
        t_transpose(1, 1)
        t_copy(0, 1, 0, ACT)
        t_copy(0, 1, 1, ACT)
        perm_table(1, 1, 0, DVE)
        perm_words(1, 1, 0, 4)
        nc.scalar.copy(out=bcol2[:], in_=bias_bank[:, 8:16])
        perm_words(1, 0, 0, 4)
        relu(0, 1, 3, ACT)
        relu(0, 1, 1, ACT)
        h_inter(0, 0, 0, DVE)
        t_transpose(1, 0)
        relu(0, 1, 2, ACT)
        t_copy(1, 1, 1, ACT)
        perm_table(2, 1, 0, DVE)
        perm_table(2, 0, 0, DVE)
        t_transpose(0, 0)
        perm_table(2, 1, 1, DVE)
        t_copy(1, 0, 0, ACT)
        t_copy(1, 1, 0, ACT)
        s1(1, 1, 0, [1])
        s1(1, 1, 1, [1])
        s1(1, 1, 2, [1])
        s1(1, 1, 3, [1])
        t_copy(0, 0, 1, ACT)
        perm_table(2, 0, 1, ACT)
        h_quant(0, 0, 0)
        s1(1, 0, 0, [0])
        s1(1, 0, 0, [1])
        s1(1, 0, 0, [2])
        s1(1, 0, 0, [3])
        s1(1, 0, 1, [0])
        s1(1, 0, 1, [1])
        s1(1, 0, 1, [2])
        s1(1, 0, 1, [3])
        t_copy(0, 0, 0, ACT)
        t_copy(1, 0, 1, ACT)
        t_quant(0, 1)
        h_inter(0, 1, 0, DVE)
        h_inter(0, 1, 1, DVE)
        h_quant(0, 1, 0)
        h_quant(0, 0, 1)
        s1(1, 0, 2, [0])
        s1(1, 0, 2, [1])
        s1(1, 0, 2, [2])
        s1(1, 0, 2, [3])
        s1(1, 0, 3, [0])
        s1(1, 0, 3, [1])
        s1(1, 0, 3, [2])
        s1(1, 0, 3, [3])
        t_quant(0, 0)
        perm_table(3, 0, 0, ACT)
        t_transpose(2, 1)
        relu(1, 0, 2, ACT)
        relu(1, 0, 0, ACT)
        t_transpose(2, 0)
        t_quant(1, 1)
        s2(0, 0, 1)
        relu(1, 0, 1, ACT)
        perm_table(3, 1, 0, ACT)
        relu(1, 0, 3, ACT)
        h_quant(0, 1, 1)
        t_copy(2, 1, 1, DVE)
        t_quant(1, 0)
        s1(1, 1, 0, [0])
        s1(1, 1, 1, [0])
        s1(1, 1, 2, [0])
        s1(1, 1, 3, [0])
        perm_table(3, 0, 1, DVE)
        finish(0, 0, 1, DVE)
        s2(0, 1, 0)
        s2(0, 1, 1)
        perm_table(3, 1, 1, DVE)
        relu(1, 1, 0, ACT)
        finish(0, 1, 0, DVE)
        s2(0, 0, 0)
        finish(0, 0, 0, DVE)
        t_transpose(3, 1)
        t_copy(2, 1, 0, ACT)
        t_transpose(3, 0)
        relu(1, 1, 1, ACT)
        t_copy(2, 0, 1, ACT)
        t_copy(2, 0, 0, ACT)
        t_copy(3, 1, 1, ACT)
        s2(0, 1, 2)
        s2(0, 0, 3)
        finish(0, 1, 1, DVE)
        t_quant(2, 1)
        t_copy(3, 0, 1, ACT)
        s1(1, 1, 0, [3])
        s1(1, 1, 1, [3])
        s1(1, 1, 2, [3])
        s1(1, 1, 3, [3])
        t_quant(2, 0)
        finish(0, 1, 2, DVE)
        finish(0, 0, 3, DVE)
        t_copy(3, 0, 0, ACT)
        s2(0, 1, 3)
        s2(0, 0, 2)
        t_copy(3, 1, 0, ACT)
        h_inter(1, 0, 0, ACT)
        t_quant(3, 1)
        s1(1, 1, 0, [2])
        s1(1, 1, 1, [2])
        s1(1, 1, 2, [2])
        s1(1, 1, 3, [2])
        t_quant(3, 0)
        s2(0, 2, 0)
        s2(0, 3, 0)
        relu(1, 1, 3, ACT)
        finish(0, 0, 2, DVE)
        relu(1, 1, 2, ACT)
        h_quant(1, 0, 0)
        s2(0, 3, 2)
        s2(0, 2, 2)
        s2(0, 3, 1)
        finish(0, 1, 3, DVE)
        finish(0, 2, 0, DVE)
        finish(0, 3, 0, DVE)
        h_inter(1, 1, 0, ACT)
        finish(0, 3, 2, DVE)
        h_quant(1, 1, 0)
        h_inter(1, 1, 1, ACT)
        s2(0, 2, 1)
        s2(1, 1, 0)
        finish(0, 2, 2, DVE)
        s2(0, 2, 3)
        s2(1, 0, 0)
        finish(0, 2, 1, DVE)
        s2(0, 3, 3)
        finish(0, 3, 1, DVE)
        s2(1, 1, 1)
        s2(1, 0, 1)
        finish(0, 2, 3, DVE)
        finish(1, 1, 0, ACT)
        finish(1, 0, 0, DVE)
        h_inter(1, 0, 1, ACT)
        h_quant(1, 0, 1)
        finish(0, 3, 3, DVE)
        s2(1, 3, 0)
        h_quant(1, 1, 1)
        s2(1, 3, 1)
        finish(1, 1, 1, ACT)
        finish(1, 0, 1, DVE)
        s2(1, 2, 0)
        finish(1, 3, 0, ACT)
        s2(1, 1, 2)
        s2(1, 2, 1)
        s2(1, 2, 2)
        s2(1, 2, 3)
        s2(1, 0, 2)
        finish(1, 2, 0, DVE)
        s2(1, 1, 3)
        finish(1, 2, 1, DVE)
        finish(1, 2, 3, DVE)
        finish(1, 2, 2, DVE)
        s2(1, 3, 2)
        s2(1, 0, 3)
        finish(1, 3, 1, ACT)
        s2(1, 3, 3)
        finish(1, 1, 2, ACT)
        finish(1, 0, 2, DVE)
        finish(1, 1, 3, DVE)
        finish(1, 0, 3, DVE)
        finish(1, 3, 2, ACT)
        finish(1, 3, 3, DVE)
